import numpy as np
CORES = [0,1,2,3,4,5,6,7,128,129,130,131,132,133,134,135,256,257,258,259,260,261,262,263,384,385,386,387,388,389,390,391]
N = 32
def setup_inputs(rng):
    return {"x1": rng.standard_normal((N, 128, 32), dtype=np.float32), "x2": rng.standard_normal((N, 128, 512), dtype=np.float32)}
def reference(x1, x2):
    out = []
    s = x1.sum(axis=0, dtype=np.float64).astype(x1.dtype)
    out.append(np.broadcast_to(s, (N,) + s.shape))
    b = 512 // N
    bl = x2.reshape(N, 128, N, b)
    out.append(np.ascontiguousarray(bl.transpose(2, 1, 0, 3)).reshape(N, 128, 512))
    return {"y1": out[0], "y2": out[1]}

@@ -1,0 +1,97 @@
+from concourse.bass import DstId, RemoteDMATransfer
+
+B = 16
+NC = 8
+NH = 4
+
+SCRATCH = {
+    "sx2": ("sbuf", [128, 512], "float32"),
+    "land2": ("sbuf", [128, 512], "float32"),
+    "relay": ("sbuf", [128, 128], "float32"),
+    "d1": ("dram", [8, 128, 4], "float32"),
+    "g1": ("dram", [16, 128, 4], "float32"),
+    "p1": ("dram", [128, 4], "float32"),
+    "o1": ("dram", [8, 128, 4], "float32"),
+}
+SEMAPHORES = ["ld1", "ld2", "rs1", "pr1", "fin1", "rel2", "arr2", "sent", "st1", "st2"]
+
+
+def rank_program(g, core, T, topo):
+    rank = T.rank_of(core)
+    if rank is None:
+        return
+    S = T.sem
+    h, c = rank // NC, rank % NC
+    rackp, cablep = h ^ 1, 3 - h
+
+    def world(host, k):
+        return T.cores[host * NC + k]
+
+    def dst_id(host, k):
+        rid, pid = topo.addr(world(host, k), core)
+        return DstId(rid=rid, pnc=pid)
+
+    def blk(t, j, n=1):
+        return t[:, j * B:(j + n) * B]
+
+    sent = [0]
+
+    def fused(transfers, engines):
+        g.remote_dma_fused(transfers, local_sem=S.sent)
+        sent[0] += engines
+
+    g.scalar.dma_start(T.d1[:], T.x1[:]).then_inc(S.ld1, 16)
+    g.sync.dma_start(T.sx2[:], T.x2[:]).then_inc(S.ld2, 16)
+    g.sync.dma_start(blk(T.land2, rank), blk(T.x2, rank)).then_inc(S.arr2, 16)
+
+    g.wait_ge(S.ld1, 16)
+    tr, e = [], 8
+    for k in range(NC):
+        tr.append(RemoteDMATransfer(dst_ids=[dst_id(rackp, k)], dma_engine_mask=1 << k, remote_sem=S.rs1,
+                                    src=T.d1[k], dst=T.g1[NC + c]))
+        if k != c:
+            tr.append(RemoteDMATransfer(dst_ids=[dst_id(h, k)], dma_engine_mask=1 << e, remote_sem=S.rs1,
+                                        src=T.d1[k], dst=T.g1[c]))
+            e += 1
+    fused(tr, len(tr))
+
+    g.wait_ge(S.ld2, 16)
+    diag = (h + 2) % NH
+    tr, e = [], 8
+    for k in range(NC):
+        via = rackp if k % 2 == 0 else cablep
+        tr.append(RemoteDMATransfer(dst_ids=[dst_id(via, k)], dma_engine_mask=1 << k, remote_sem=S.rel2,
+                                    src=blk(T.sx2, diag * NC + k), dst=blk(T.relay, c)))
+        if k != c:
+            tr.append(RemoteDMATransfer(dst_ids=[dst_id(h, k)], dma_engine_mask=1 << e, remote_sem=S.arr2,
+                                        src=blk(T.sx2, h * NC + k), dst=blk(T.land2, rank)))
+            e += 1
+    fused(tr, len(tr))
+    for hn in (rackp, cablep):
+        fused([RemoteDMATransfer(dst_ids=[dst_id(hn, k)], dma_engine_mask=1 << k, remote_sem=S.arr2,
+                                 src=blk(T.sx2, hn * NC + k), dst=blk(T.land2, rank)) for k in range(NC)], NC)
+
+    g.wait_ge(S.rs1, 15)
+    mine = [T.d1[c]] + [T.g1[k] for k in range(2 * NC) if k != c]
+    fused([RemoteDMATransfer(dst_ids=[dst_id(cablep, c)], dma_engine_mask=1, remote_sem=S.pr1,
+                             srcs=mine, dsts=[T.p1[:]], alu_op=1)], 1)
+
+    g.wait_ge(S.rel2, NC)
+    hs, hd = (rackp, cablep) if c % 2 == 0 else (cablep, rackp)
+    rid, pid = topo.addr(world(hd, c), core)
+    g.remote_dma(blk(T.land2, hs * NC, NC), T.relay[:], S.arr2, S.sent, pid, rid, 0xFF)
+    sent[0] += 8
+
+    g.wait_ge(S.pr1, 1)
+    to = [dst_id(h, k) for k in range(NC) if k != c] + [dst_id(cablep, c)]
+    fused([RemoteDMATransfer(dst_ids=to, dma_engine_mask=1, remote_sem=S.fin1,
+                             srcs=mine + [T.p1[:]], dsts=[T.o1[c]] * len(to), alu_op=1)], 1)
+
+    g.scalar.wait_ge(S.fin1, NC)
+    g.scalar.dma_start(T.y1[:], T.o1[:]).then_inc(S.st1, 16)
+    g.sync.wait_ge(S.arr2, 16 + 7 + 16 + 8)
+    g.sync.dma_start(T.y2[:], T.land2[:]).then_inc(S.st2, 16)
+
+    g.wait_ge(S.sent, sent[0])
+    g.wait_ge(S.st1, 16)
+    g.wait_ge(S.st2, 16)

@@ -22,7 +22,7 @@ def rank_program(g, core, T, topo):
         return
     S = T.sem
     h, c = rank // NC, rank % NC
-    rackp, cablep = h ^ 1, 3 - h
+    rackp, cablep, diag = h ^ 1, 3 - h, (h + 2) % NH
 
     def world(host, k):
         return T.cores[host * NC + k]
@@ -36,9 +36,13 @@ def rank_program(g, core, T, topo):
 
     sent = [0]
 
-    def fused(transfers, engines):
+    def fused(transfers):
         g.remote_dma_fused(transfers, local_sem=S.sent)
-        sent[0] += engines
+        sent[0] += len(transfers)
+
+    def to_host(hn):
+        fused([RemoteDMATransfer(dst_ids=[dst_id(hn, k)], dma_engine_mask=1 << k, remote_sem=S.arr2,
+                                 src=blk(T.sx2, hn * NC + k), dst=blk(T.land2, rank)) for k in range(NC)])
 
     g.scalar.dma_start(T.d1[:], T.x1[:]).then_inc(S.ld1, 16)
     g.sync.dma_start(T.sx2[:], T.x2[:]).then_inc(S.ld2, 16)
@@ -53,10 +57,9 @@ def rank_program(g, core, T, topo):
             tr.append(RemoteDMATransfer(dst_ids=[dst_id(h, k)], dma_engine_mask=1 << e, remote_sem=S.rs1,
                                         src=T.d1[k], dst=T.g1[c]))
             e += 1
-    fused(tr, len(tr))
+    fused(tr)
 
     g.wait_ge(S.ld2, 16)
-    diag = (h + 2) % NH
     tr, e = [], 8
     for k in range(NC):
         via = rackp if k % 2 == 0 else cablep
@@ -66,26 +69,29 @@ def rank_program(g, core, T, topo):
             tr.append(RemoteDMATransfer(dst_ids=[dst_id(h, k)], dma_engine_mask=1 << e, remote_sem=S.arr2,
                                         src=blk(T.sx2, h * NC + k), dst=blk(T.land2, rank)))
             e += 1
-    fused(tr, len(tr))
-    for hn in (rackp, cablep):
-        fused([RemoteDMATransfer(dst_ids=[dst_id(hn, k)], dma_engine_mask=1 << k, remote_sem=S.arr2,
-                                 src=blk(T.sx2, hn * NC + k), dst=blk(T.land2, rank)) for k in range(NC)], NC)
+    fused(tr)
 
     g.wait_ge(S.rs1, 15)
     mine = [T.d1[c]] + [T.g1[k] for k in range(2 * NC) if k != c]
     fused([RemoteDMATransfer(dst_ids=[dst_id(cablep, c)], dma_engine_mask=1, remote_sem=S.pr1,
-                             srcs=mine, dsts=[T.p1[:]], alu_op=1)], 1)
+                             srcs=mine, dsts=[T.p1[:]], alu_op=1)])
+
+    to_host(rackp)
+
+    g.wait_ge(S.pr1, 1)
+    chip = [dst_id(h, k) for k in range(NC) if k != c]
+    fused([RemoteDMATransfer(dst_ids=chip, dma_engine_mask=1 << 15, remote_sem=S.fin1,
+                             srcs=mine + [T.p1[:]], dsts=[T.o1[c]] * len(chip), alu_op=1),
+           RemoteDMATransfer(dst_ids=[dst_id(rackp, c)], dma_engine_mask=1, remote_sem=S.fin1,
+                             srcs=mine + [T.p1[:]], dsts=[T.o1[c]], alu_op=1)])
+
+    to_host(cablep)
 
     g.wait_ge(S.rel2, NC)
     hs, hd = (rackp, cablep) if c % 2 == 0 else (cablep, rackp)
     rid, pid = topo.addr(world(hd, c), core)
     g.remote_dma(blk(T.land2, hs * NC, NC), T.relay[:], S.arr2, S.sent, pid, rid, 0xFF)
     sent[0] += 8
-
-    g.wait_ge(S.pr1, 1)
-    to = [dst_id(h, k) for k in range(NC) if k != c] + [dst_id(cablep, c)]
-    fused([RemoteDMATransfer(dst_ids=to, dma_engine_mask=1, remote_sem=S.fin1,
-                             srcs=mine + [T.p1[:]], dsts=[T.o1[c]] * len(to), alu_op=1)], 1)
 
     g.scalar.wait_ge(S.fin1, NC)
     g.scalar.dma_start(T.y1[:], T.o1[:]).then_inc(S.st1, 16)

from concourse.bass import DstId, RemoteDMATransfer

B = 16
NC = 8
NH = 4

SCRATCH = {
    "sx2": ("sbuf", [128, 512], "float32"),
    "land2": ("sbuf", [128, 512], "float32"),
    "relay": ("sbuf", [128, 128], "float32"),
    "d1": ("dram", [8, 128, 4], "float32"),
    "g1": ("dram", [16, 128, 4], "float32"),
    "p1": ("dram", [128, 4], "float32"),
    "o1": ("dram", [8, 128, 4], "float32"),
}
SEMAPHORES = ["ld1", "ld2", "rs1", "pr1", "fin1", "rel2", "arr2", "sent", "st1", "st2"]


def rank_program(g, core, T, topo):
    rank = T.rank_of(core)
    if rank is None:
        return
    S = T.sem
    h, c = rank // NC, rank % NC
    rackp, cablep, diag = h ^ 1, 3 - h, (h + 2) % NH

    def world(host, k):
        return T.cores[host * NC + k]

    def dst_id(host, k):
        rid, pid = topo.addr(world(host, k), core)
        return DstId(rid=rid, pnc=pid)

    def blk(t, j, n=1):
        return t[:, j * B:(j + n) * B]

    sent = [0]

    def fused(transfers):
        g.remote_dma_fused(transfers, local_sem=S.sent)
        sent[0] += len(transfers)

    def to_host(hn):
        fused([RemoteDMATransfer(dst_ids=[dst_id(hn, k)], dma_engine_mask=1 << k, remote_sem=S.arr2,
                                 src=blk(T.sx2, hn * NC + k), dst=blk(T.land2, rank)) for k in range(NC)])

    g.scalar.dma_start(T.d1[:], T.x1[:]).then_inc(S.ld1, 16)
    g.sync.dma_start(T.sx2[:], T.x2[:]).then_inc(S.ld2, 16)
    g.sync.dma_start(blk(T.land2, rank), blk(T.x2, rank)).then_inc(S.arr2, 16)

    g.wait_ge(S.ld1, 16)
    tr, e = [], 8
    for k in range(NC):
        tr.append(RemoteDMATransfer(dst_ids=[dst_id(rackp, k)], dma_engine_mask=1 << k, remote_sem=S.rs1,
                                    src=T.d1[k], dst=T.g1[NC + c]))
        if k != c:
            tr.append(RemoteDMATransfer(dst_ids=[dst_id(h, k)], dma_engine_mask=1 << e, remote_sem=S.rs1,
                                        src=T.d1[k], dst=T.g1[c]))
            e += 1
    fused(tr)

    g.wait_ge(S.ld2, 16)
    tr, e = [], 8
    for k in range(NC):
        via = rackp if k % 2 == 0 else cablep
        tr.append(RemoteDMATransfer(dst_ids=[dst_id(via, k)], dma_engine_mask=1 << k, remote_sem=S.rel2,
                                    src=blk(T.sx2, diag * NC + k), dst=blk(T.relay, c)))
        if k != c:
            tr.append(RemoteDMATransfer(dst_ids=[dst_id(h, k)], dma_engine_mask=1 << e, remote_sem=S.arr2,
                                        src=blk(T.sx2, h * NC + k), dst=blk(T.land2, rank)))
            e += 1
    fused(tr)

    g.wait_ge(S.rs1, 15)
    mine = [T.d1[c]] + [T.g1[k] for k in range(2 * NC) if k != c]
    fused([RemoteDMATransfer(dst_ids=[dst_id(cablep, c)], dma_engine_mask=1, remote_sem=S.pr1,
                             srcs=mine, dsts=[T.p1[:]], alu_op=1)])

    to_host(rackp)

    g.wait_ge(S.pr1, 1)
    chip = [dst_id(h, k) for k in range(NC) if k != c]
    fused([RemoteDMATransfer(dst_ids=chip, dma_engine_mask=1 << 15, remote_sem=S.fin1,
                             srcs=mine + [T.p1[:]], dsts=[T.o1[c]] * len(chip), alu_op=1),
           RemoteDMATransfer(dst_ids=[dst_id(rackp, c)], dma_engine_mask=1, remote_sem=S.fin1,
                             srcs=mine + [T.p1[:]], dsts=[T.o1[c]], alu_op=1)])

    to_host(cablep)

    g.wait_ge(S.rel2, NC)
    hs, hd = (rackp, cablep) if c % 2 == 0 else (cablep, rackp)
    rid, pid = topo.addr(world(hd, c), core)
    g.remote_dma(blk(T.land2, hs * NC, NC), T.relay[:], S.arr2, S.sent, pid, rid, 0xFF)
    sent[0] += 8

    g.scalar.wait_ge(S.fin1, NC)
    g.scalar.dma_start(T.y1[:], T.o1[:]).then_inc(S.st1, 16)
    g.sync.wait_ge(S.arr2, 16 + 7 + 16 + 8)
    g.sync.dma_start(T.y2[:], T.land2[:]).then_inc(S.st2, 16)

    g.wait_ge(S.sent, sent[0])
    g.wait_ge(S.st1, 16)
    g.wait_ge(S.st2, 16)
